import numpy as np
import ml_dtypes


def mxq(x, axis, fmt="e4m3"):
    dtype, down = {"e4m3": (ml_dtypes.float8_e4m3fn, 7), "e5m2": (ml_dtypes.float8_e5m2, 14)}[fmt]
    v = np.moveaxis(np.asarray(x, np.float32).astype(ml_dtypes.bfloat16).astype(np.float64), axis, -1)
    blocks = v.reshape(v.shape[:-1] + (-1, 32))
    amax = np.abs(blocks).max(-1, keepdims=True)
    byte = np.maximum(np.where(amax > 0, np.frexp(amax)[1] - 1 + 127, 0) - down, 1)
    scale = np.exp2(byte - 127.0)
    codes = (blocks / scale).astype(np.float32).astype(dtype).astype(np.float64)
    return np.moveaxis((codes * scale).reshape(v.shape), -1, axis)


WIDE = False


def mx_kscale(k):
    if not WIDE:
        return np.ones(k)
    levels = np.array([10, -10, 5, -5, 0])
    if k % 512:
        return np.exp2(np.random.permutation(np.resize(levels, k // 32))).repeat(32)
    a = np.empty((k // 512, 16))
    for p in range(k // 512):
        a[p, :8] = np.random.permutation(np.resize(levels, 8))
        for g in range(8):
            far = levels[np.abs(levels - a[p, g]) >= 10]
            a[p, g + 8] = far[np.random.randint(len(far))]
    return np.exp2(a.ravel()).repeat(32)


def f64(x):
    return np.asarray(x).astype(np.float64)


def striped(idx):
    return np.tile(idx.reshape(-1, 16).T, (8, 1)).astype(np.uint16)


def unstriped(offs):
    return offs[:16].T.reshape(-1).astype(np.int64)


def striped8(idx):
    return np.concatenate([x.reshape(-1, 16).T for x in idx]).astype(np.uint16)


def runs(offs, k):
    lists = np.stack([offs[16 * r : 16 * r + 16].T.reshape(-1) for r in range(8)]).astype(np.int64)
    return lists[np.arange(k) % 512 // 64]


def pack_weight(w):
    k, n = w.shape
    w = f64(np.asarray(w, np.float32).astype(ml_dtypes.bfloat16)).reshape(k // 32, 32, n)
    amax = np.abs(w).max(1)
    byte = np.clip(np.where(amax > 0, np.frexp(amax)[1] - 1 + 127 - 7, 1), 1, 254)
    scaled = (w * np.exp2(127.0 - byte)[:, None, :]).reshape(k, n).astype(np.float32)
    words = np.ascontiguousarray(scaled.reshape(k // 512, 128, 4, n).transpose(0, 1, 3, 2)).astype(ml_dtypes.float8_e4m3fn).view(np.uint8)
    return words, np.ascontiguousarray(byte.astype(np.uint8).reshape(k // 512, 16, n))


def unpack_weight(words, scales):
    g, p, n, _ = words.shape
    vals = np.ascontiguousarray(words).view(ml_dtypes.float8_e4m3fn).astype(np.float64) * np.repeat(np.exp2(scales.astype(np.float64) - 127.0), 8, axis=1)[..., None]
    return vals.transpose(0, 1, 3, 2).reshape(g * 512, n)


def relu(v):
    return np.maximum(v, 0.0)


K, T, S, V, H = 512, 2048, 512, 512, 512


def setup_inputs():
    n = np.random.standard_normal
    s = mx_kscale(K)[:, None]
    u = mx_kscale(H)
    packed_xT = pack_weight(n((K, T)) * s)
    return {
        "x_words": packed_xT[0],
        "x_scales": packed_xT[1],
        "w1": (n((K, H)) / np.sqrt(K) / s * u).astype(np.float32),
        "w2": (n((H, H)) / np.sqrt(H) / u[:, None]).astype(np.float32),
        "gs": (np.random.uniform(0.5, 1.5, (K, 1)) / s).astype(np.float32),
        "pri": n((V, S)).astype(np.float32),
        "offs": striped(np.random.permutation(T)[:S]),
        "nb": striped8(np.stack([np.random.permutation(S) for _ in range(8)])),
        "cand": striped(np.random.permutation(T)[:V]),
    }


def reference(x_words, x_scales, w1, w2, gs, pri, offs, nb, cand):
    x_cand = unpack_weight(x_words, x_scales)[:, unstriped(cand)]
    xq = unpack_weight(x_words, x_scales)[:, unstriped(offs)]
    h = mxq(f64(w1), 0, "e4m3").T @ xq
    z = h[np.arange(H)[:, None], runs(nb, H)]
    h2 = relu(mxq(f64(w2), 0, "e4m3").T @ mxq(z, 0, "e4m3"))
    z2 = f64(gs) * h2
    return f64(pri) + 0.0625 * ((x_cand.T @ mxq(z2, 0, "e4m3")))

@@ -1,0 +1,173 @@
+from contextlib import ExitStack
+
+import concourse.mybir as mybir
+
+K, T, S, V, H = 512, 2048, 512, 512, 512
+FLOPS = 2 * K * H * S + 2 * H * H * S + 2 * K * V * S
+
+F32 = mybir.dt.float32
+BF16 = mybir.dt.bfloat16
+I32 = mybir.dt.int32
+U32 = mybir.dt.uint32
+U16 = mybir.dt.uint16
+U8 = mybir.dt.uint8
+FP8X4 = mybir.dt.float8_e4m3fn_x4
+ALU = mybir.AluOpType
+
+P = 128
+PACK = 4
+HALF = 256
+PART = 128
+
+
+def tile_picked_candnbr_relu_p_kernel(tc, x_words, x_scales, w1, w2, gs, pri, offs, nb, cand, out):
+    nc = tc.nc
+    with ExitStack() as ctx:
+        keep = ctx.enter_context(tc.tile_pool(name="keep", bufs=1))
+        psum = ctx.enter_context(tc.psum_pool(name="psum", bufs=4))
+
+        def sb(name, shape, dtype, tag=None):
+            return keep.tile(shape, dtype, name=name, tag=tag or name, align_bytes=64)
+
+        def load_half(name, w, u):
+            raw = sb(name, [P, PACK, HALF], F32)
+            nc.sync.dma_start(out=raw[:], in_=w.rearrange("(p j) c -> p j c", j=PACK)[:, :, u * HALF : (u + 1) * HALF])
+            return raw
+
+        offs_t = sb("offs_t", [P, S // 16], U16)
+        cand_t = sb("cand_t", [P, V // 16], U16)
+        nb_t = sb("nb_t", [P, S // 16], U16)
+        xw = sb("xw", [P, T], U32)
+        xs = sb("xs", [P, T], U8)
+        nc.vector.memset(xs[:].bitcast(I32), 0)
+        nc.sync.dma_start(offs_t[:], offs)
+        nc.sync.dma_start(cand_t[:], cand)
+        w1_raw = [load_half("w1_raw0", w1, 0)]
+        for q in range(4):
+            nc.sync.dma_start(out=xs[32 * q : 32 * q + 4, :].bitcast(I32), in_=x_scales[0, 4 * q : 4 * q + 4, :].bitcast(I32))
+        nc.sync.dma_start(out=xw[:].bitcast(I32), in_=x_words[0].rearrange("p n t -> p (n t)").bitcast(I32))
+        w1_raw.append(load_half("w1_raw1", w1, 1))
+        nc.sync.dma_start(nb_t[:], nb)
+        w2_raw = [load_half("w2_raw%d" % u, w2, u) for u in range(2)]
+        gs_t = sb("gs_t", [P, PACK], F32)
+        nc.sync.dma_start(out=gs_t[:], in_=gs.rearrange("(p t) o -> p (t o)", t=PACK))
+        pri_t = []
+        for u in range(2):
+            pt = sb("pri%d" % u, [P, PACK, HALF], F32)
+            nc.sync.dma_start(out=pt[:], in_=pri.rearrange("(v p) s -> p v s", p=P)[:, :, u * HALF : (u + 1) * HALF])
+            pri_t.append(pt)
+
+        def deal(copy, grouped, raw, u, m0, m1):
+            copy(
+                out=grouped[:, :, 64 * u + m0 : 64 * u + m1, :].rearrange("p t m j -> p m j t"),
+                in_=raw[:, :, PACK * m0 : PACK * m1].rearrange("p j (m t) -> p m j t", t=PACK),
+            )
+
+        def quantise(codes, scales, values):
+            nc.vector.quantize_mx(out=codes.bitcast(FP8X4), scales=scales, in_=values)
+
+        def product(acc, lhs_c, lhs_s, rhs_c, rhs_s):
+            nc.tensor.matmul_mx(out=acc, lhsT=lhs_c.bitcast(FP8X4), lhsT_scale=lhs_s, rhs=rhs_c.bitcast(FP8X4), rhs_scale=rhs_s, start=True, stop=True)
+
+        xq_w = sb("xq_w", [P, S], U32)
+        xq_s = sb("xq_s", [P, S], U8)
+        xc_s = sb("xc_s", [P, V], U8)
+        nc.vector.tensor_copy(xq_s[:], xs[:].indirect(offs_t[:]))
+        nc.vector.tensor_copy(xc_s[:], xs[:].indirect(cand_t[:]))
+        nc.vector.tensor_copy(xq_w[:], xw[:].indirect(offs_t[:]))
+
+        g1 = sb("g1", [P, PACK, P, PACK], BF16)
+        deal(nc.scalar.copy, g1, w1_raw[0], 0, 0, 64)
+        deal(nc.scalar.copy, g1, w1_raw[1], 1, 0, 24)
+        deal(nc.vector.tensor_copy, g1, w1_raw[1], 1, 24, 64)
+        w1_c = sb("w1_c", [P, H], U32)
+        w1_s = sb("w1_s", [P, H], U8)
+        h = []
+        for t in range(PACK):
+            cols = slice(P * t, P * (t + 1))
+            quantise(w1_c[:, cols], w1_s[:, cols], g1[:, t].rearrange("p m j -> p (m j)"))
+            bank = psum.tile([P, S], F32, name="wide")
+            product(bank[:], w1_c[:, cols], w1_s[:, cols], xq_w[:], xq_s[:])
+            ht = sb("h%d" % t, [P, S], F32)
+            nc.scalar.copy(out=ht[:], in_=bank[:])
+            h.append(ht)
+        xc_w = sb("xc_w", [P, V], U32, tag="g1")
+        nc.vector.tensor_copy(xc_w[:], xw[:].indirect(cand_t[:]))
+
+        g2 = sb("g2", [P, PACK, P, PACK], BF16, tag="xq_w")
+        deal(nc.scalar.copy, g2, w2_raw[0], 0, 0, 64)
+        deal(nc.scalar.copy, g2, w2_raw[1], 1, 0, 64)
+
+        w2_c = sb("w2_c", [P, H], U32)
+        w2_s = sb("w2_s", [P, H], U8)
+        zi = sb("zi", [P, S, PACK], BF16)
+        z_c = sb("z_c", [P, S], U32)
+        z_s = sb("z_s", [P, S], U8)
+
+        def fetch(name, tag, c0, c1):
+            planes = sb(name, [P, PACK, c1 - c0], BF16, tag=tag)
+            for t in range(PACK):
+                nc.vector.tensor_copy(planes[:, t, :], h[t][:].indirect(nb_t[:, c0 // 16 : c1 // 16]))
+            nc.scalar.copy(out=zi[:, c0:c1, :].rearrange("p (c i) t -> p c t i", i=4), in_=planes[:].rearrange("p t (c i) -> p c t i", i=4))
+
+        def quant_z(c0, c1):
+            quantise(z_c[:, c0:c1], z_s[:, c0:c1], zi[:, c0:c1, :].rearrange("p c t -> p (c t)"))
+
+        second = {}
+
+        def layer2(c):
+            cols = slice(PART * c, PART * (c + 1))
+            bank = psum.tile([P, PACK, PART], F32, name="second")
+            for t in range(PACK):
+                wc = slice(P * t, P * (t + 1))
+                product(bank[:, t, :], w2_c[:, wc], w2_s[:, wc], z_c[:, cols], z_s[:, cols])
+            second[c] = bank
+
+        z2 = [sb("z2_%d" % c, [P, PART, PACK], BF16) for c in range(4)]
+        z2_c = [sb("z2_c%d" % c, [P, PART], U32) for c in range(4)]
+        z2_s = [sb("z2_s%d" % c, [P, PART], U8) for c in range(4)]
+
+        def weigh(c):
+            nc.vector.scalar_tensor_tensor(
+                out=z2[c][:], in0=second[c][:].rearrange("p t n -> p n t"), scalar=0.0,
+                in1=gs_t[:].unsqueeze(1).to_broadcast([P, PART, PACK]), op0=ALU.max, op1=ALU.mult)
+
+        third = {}
+
+        def score(c):
+            quantise(z2_c[c][:], z2_s[c][:], z2[c][:].rearrange("p n t -> p (n t)"))
+            bank = psum.tile([P, PACK, PART], F32, name="wide")
+            for v in range(PACK):
+                vc = slice(P * v, P * (v + 1))
+                product(bank[:, v, :], xc_w[:, vc], xc_s[:, vc], z2_c[c][:], z2_s[c][:])
+            third[c] = bank
+
+        def finish(c):
+            u, a = divmod(c, 2)
+            res = sb("res%d" % c, [P, PACK, PART], F32)
+            nc.vector.scalar_tensor_tensor(out=res[:], in0=third[c][:], scalar=0.0625, in1=pri_t[u][:, :, PART * a : PART * (a + 1)], op0=ALU.mult, op1=ALU.add)
+            nc.sync.dma_start(out=out.rearrange("(v p) s -> p v s", p=P)[:, :, PART * c : PART * (c + 1)], in_=res[:])
+
+        fetch("zp_a", "zp_a", 0, 256)
+        fetch("zp_b", "w2_raw0", 256, 384)
+        quantise(w2_c[:], w2_s[:], g2[:].rearrange("p t m j -> p (t m j)"))
+        quant_z(0, 256)
+        layer2(0)
+        layer2(1)
+        fetch("zp_c", "zp_a", 384, 512)
+        quant_z(256, 384)
+        layer2(2)
+        weigh(0)
+        weigh(1)
+        quant_z(384, 512)
+        layer2(3)
+        score(0)
+        weigh(2)
+        score(1)
+        weigh(3)
+        finish(0)
+        score(2)
+        finish(1)
+        score(3)
+        finish(2)
+        finish(3)

@@ -29,9 +29,9 @@ def tile_picked_candnbr_relu_p_kernel(tc, x_words, x_scales, w1, w2, gs, pri, of
         def sb(name, shape, dtype, tag=None):
             return keep.tile(shape, dtype, name=name, tag=tag or name, align_bytes=64)
 
-        def load_half(name, w, u):
-            raw = sb(name, [P, PACK, HALF], F32)
-            nc.sync.dma_start(out=raw[:], in_=w.rearrange("(p j) c -> p j c", j=PACK)[:, :, u * HALF : (u + 1) * HALF])
+        def load_cols(name, w, c0, c1):
+            raw = sb(name, [P, PACK, c1 - c0], F32)
+            nc.sync.dma_start(out=raw[:], in_=w.rearrange("(p j) c -> p j c", j=PACK)[:, :, c0:c1])
             return raw
 
         offs_t = sb("offs_t", [P, S // 16], U16)
@@ -42,13 +42,15 @@ def tile_picked_candnbr_relu_p_kernel(tc, x_words, x_scales, w1, w2, gs, pri, of
         nc.vector.memset(xs[:].bitcast(I32), 0)
         nc.sync.dma_start(offs_t[:], offs)
         nc.sync.dma_start(cand_t[:], cand)
-        w1_raw = [load_half("w1_raw0", w1, 0)]
+        w1_a = load_cols("w1_a", w1, 0, 256)
         for q in range(4):
             nc.sync.dma_start(out=xs[32 * q : 32 * q + 4, :].bitcast(I32), in_=x_scales[0, 4 * q : 4 * q + 4, :].bitcast(I32))
+        w1_b = load_cols("w1_b", w1, 256, 512)
         nc.sync.dma_start(out=xw[:].bitcast(I32), in_=x_words[0].rearrange("p n t -> p (n t)").bitcast(I32))
-        w1_raw.append(load_half("w1_raw1", w1, 1))
         nc.sync.dma_start(nb_t[:], nb)
-        w2_raw = [load_half("w2_raw%d" % u, w2, u) for u in range(2)]
+        w2_a = load_cols("w2_a", w2, 0, 128)
+        w2_c3 = load_cols("w2_c3", w2, 256, 512)
+        w2_b = load_cols("w2_b", w2, 128, 256)
         gs_t = sb("gs_t", [P, PACK], F32)
         nc.sync.dma_start(out=gs_t[:], in_=gs.rearrange("(p t) o -> p (t o)", t=PACK))
         pri_t = []
@@ -57,11 +59,9 @@ def tile_picked_candnbr_relu_p_kernel(tc, x_words, x_scales, w1, w2, gs, pri, of
             nc.sync.dma_start(out=pt[:], in_=pri.rearrange("(v p) s -> p v s", p=P)[:, :, u * HALF : (u + 1) * HALF])
             pri_t.append(pt)
 
-        def deal(copy, grouped, raw, u, m0, m1):
-            copy(
-                out=grouped[:, :, 64 * u + m0 : 64 * u + m1, :].rearrange("p t m j -> p m j t"),
-                in_=raw[:, :, PACK * m0 : PACK * m1].rearrange("p j (m t) -> p m j t", t=PACK),
-            )
+        def deal(copy, grouped, c0, raw):
+            m0, m1 = c0 // PACK, (c0 + raw.shape[2]) // PACK
+            copy(out=grouped[:, :, m0:m1, :].rearrange("p t m j -> p m j t"), in_=raw.rearrange("p j (m t) -> p m j t", t=PACK))
 
         def quantise(codes, scales, values):
             nc.vector.quantize_mx(out=codes.bitcast(FP8X4), scales=scales, in_=values)
@@ -74,29 +74,33 @@ def tile_picked_candnbr_relu_p_kernel(tc, x_words, x_scales, w1, w2, gs, pri, of
         xc_s = sb("xc_s", [P, V], U8)
         nc.vector.tensor_copy(xq_s[:], xs[:].indirect(offs_t[:]))
         nc.vector.tensor_copy(xc_s[:], xs[:].indirect(cand_t[:]))
-        nc.vector.tensor_copy(xq_w[:], xw[:].indirect(offs_t[:]))
 
         g1 = sb("g1", [P, PACK, P, PACK], BF16)
-        deal(nc.scalar.copy, g1, w1_raw[0], 0, 0, 64)
-        deal(nc.scalar.copy, g1, w1_raw[1], 1, 0, 24)
-        deal(nc.vector.tensor_copy, g1, w1_raw[1], 1, 24, 64)
+        deal(nc.scalar.copy, g1, 0, w1_a[:])
+        deal(nc.scalar.copy, g1, 256, w1_b[:])
         w1_c = sb("w1_c", [P, H], U32)
         w1_s = sb("w1_s", [P, H], U8)
+        quantise(w1_c[:], w1_s[:], g1[:].rearrange("p t m j -> p (t m j)"))
+        for u in range(2):
+            nc.vector.tensor_copy(xq_w[:, HALF * u : HALF * (u + 1)], xw[:].indirect(offs_t[:, 16 * u : 16 * (u + 1)]))
+        xc_w = sb("xc_w", [P, V], U32)
+        nc.vector.tensor_copy(xc_w[:], xw[:].indirect(cand_t[:]))
+
+        g2 = sb("g2", [P, PACK, P, PACK], BF16)
+        deal(nc.scalar.copy, g2, 0, w2_a[:])
         h = []
         for t in range(PACK):
             cols = slice(P * t, P * (t + 1))
-            quantise(w1_c[:, cols], w1_s[:, cols], g1[:, t].rearrange("p m j -> p (m j)"))
-            bank = psum.tile([P, S], F32, name="wide")
-            product(bank[:], w1_c[:, cols], w1_s[:, cols], xq_w[:], xq_s[:])
             ht = sb("h%d" % t, [P, S], F32)
-            nc.scalar.copy(out=ht[:], in_=bank[:])
+            width = HALF if t == 0 else S
+            for c0 in range(0, S, width):
+                bank = psum.tile([P, width], F32, name="wide")
+                product(bank[:], w1_c[:, cols], w1_s[:, cols], xq_w[:, c0 : c0 + width], xq_s[:, c0 : c0 + width])
+                nc.scalar.copy(out=ht[:, c0 : c0 + width], in_=bank[:])
             h.append(ht)
-        xc_w = sb("xc_w", [P, V], U32, tag="g1")
-        nc.vector.tensor_copy(xc_w[:], xw[:].indirect(cand_t[:]))
 
-        g2 = sb("g2", [P, PACK, P, PACK], BF16, tag="xq_w")
-        deal(nc.scalar.copy, g2, w2_raw[0], 0, 0, 64)
-        deal(nc.scalar.copy, g2, w2_raw[1], 1, 0, 64)
+        deal(nc.scalar.copy, g2, 128, w2_b[:])
+        deal(nc.scalar.copy, g2, 256, w2_c3[:])
 
         w2_c = sb("w2_c", [P, H], U32)
         w2_s = sb("w2_s", [P, H], U8)
@@ -123,33 +127,34 @@ def tile_picked_candnbr_relu_p_kernel(tc, x_words, x_scales, w1, w2, gs, pri, of
                 product(bank[:, t, :], w2_c[:, wc], w2_s[:, wc], z_c[:, cols], z_s[:, cols])
             second[c] = bank
 
-        z2 = [sb("z2_%d" % c, [P, PART, PACK], BF16) for c in range(4)]
-        z2_c = [sb("z2_c%d" % c, [P, PART], U32) for c in range(4)]
-        z2_s = [sb("z2_s%d" % c, [P, PART], U8) for c in range(4)]
+        z2 = [sb("z2_%d" % u, [P, HALF, PACK], BF16) for u in range(2)]
+        z2_c = [sb("z2_c%d" % u, [P, HALF], U32) for u in range(2)]
+        z2_s = [sb("z2_s%d" % u, [P, HALF], U8) for u in range(2)]
 
         def weigh(c):
+            u, a = divmod(c, 2)
             nc.vector.scalar_tensor_tensor(
-                out=z2[c][:], in0=second[c][:].rearrange("p t n -> p n t"), scalar=0.0,
+                out=z2[u][:, PART * a : PART * (a + 1), :], in0=second[c][:].rearrange("p t n -> p n t"), scalar=0.0,
                 in1=gs_t[:].unsqueeze(1).to_broadcast([P, PART, PACK]), op0=ALU.max, op1=ALU.mult)
 
         third = {}
 
-        def score(c):
-            quantise(z2_c[c][:], z2_s[c][:], z2[c][:].rearrange("p n t -> p (n t)"))
-            bank = psum.tile([P, PACK, PART], F32, name="wide")
-            for v in range(PACK):
-                vc = slice(P * v, P * (v + 1))
-                product(bank[:, v, :], xc_w[:, vc], xc_s[:, vc], z2_c[c][:], z2_s[c][:])
-            third[c] = bank
+        def score(u):
+            quantise(z2_c[u][:], z2_s[u][:], z2[u][:].rearrange("p n t -> p (n t)"))
+            for pair in range(2):
+                bank = psum.tile([P, 2, HALF], F32, name="wide")
+                for a in range(2):
+                    vc = slice(HALF * pair + P * a, HALF * pair + P * (a + 1))
+                    product(bank[:, a, :], xc_w[:, vc], xc_s[:, vc], z2_c[u][:], z2_s[u][:])
+                third[u, pair] = bank
 
-        def finish(c):
-            u, a = divmod(c, 2)
-            res = sb("res%d" % c, [P, PACK, PART], F32)
-            nc.vector.scalar_tensor_tensor(out=res[:], in0=third[c][:], scalar=0.0625, in1=pri_t[u][:, :, PART * a : PART * (a + 1)], op0=ALU.mult, op1=ALU.add)
-            nc.sync.dma_start(out=out.rearrange("(v p) s -> p v s", p=P)[:, :, PART * c : PART * (c + 1)], in_=res[:])
+        def finish(u, pair):
+            res = sb("res%d_%d" % (u, pair), [P, 2, HALF], F32)
+            nc.vector.scalar_tensor_tensor(out=res[:], in0=third[u, pair][:], scalar=0.0625, in1=pri_t[u][:, 2 * pair : 2 * pair + 2, :], op0=ALU.mult, op1=ALU.add)
+            nc.sync.dma_start(out=out.rearrange("(v p) s -> p v s", p=P)[:, 2 * pair : 2 * pair + 2, HALF * u : HALF * (u + 1)], in_=res[:])
 
         fetch("zp_a", "zp_a", 0, 256)
-        fetch("zp_b", "w2_raw0", 256, 384)
+        fetch("zp_b", "w2_b", 256, 384)
         quantise(w2_c[:], w2_s[:], g2[:].rearrange("p t m j -> p (t m j)"))
         quant_z(0, 256)
         layer2(0)
@@ -163,11 +168,9 @@ def tile_picked_candnbr_relu_p_kernel(tc, x_words, x_scales, w1, w2, gs, pri, of
         layer2(3)
         score(0)
         weigh(2)
-        score(1)
         weigh(3)
-        finish(0)
-        score(2)
-        finish(1)
-        score(3)
-        finish(2)
-        finish(3)
+        finish(0, 0)
+        score(1)
+        finish(0, 1)
+        finish(1, 0)
+        finish(1, 1)

@@ -92,11 +92,11 @@ def tile_picked_candnbr_relu_p_kernel(tc, x_words, x_scales, w1, w2, gs, pri, of
         for t in range(PACK):
             cols = slice(P * t, P * (t + 1))
             ht = sb("h%d" % t, [P, S], F32)
-            width = HALF if t == 0 else S
-            for c0 in range(0, S, width):
-                bank = psum.tile([P, width], F32, name="wide")
-                product(bank[:], w1_c[:, cols], w1_s[:, cols], xq_w[:, c0 : c0 + width], xq_s[:, c0 : c0 + width])
-                nc.scalar.copy(out=ht[:, c0 : c0 + width], in_=bank[:])
+            edges = (0, 256, 384, 512) if t == 0 else (0, 512)
+            for c0, c1 in zip(edges, edges[1:]):
+                bank = psum.tile([P, c1 - c0], F32, name="first", tag="wide" if c1 - c0 > PART else "second")
+                product(bank[:], w1_c[:, cols], w1_s[:, cols], xq_w[:, c0:c1], xq_s[:, c0:c1])
+                nc.scalar.copy(out=ht[:, c0:c1], in_=bank[:])
             h.append(ht)
 
         deal(nc.scalar.copy, g2, 128, w2_b[:])
@@ -112,7 +112,8 @@ def tile_picked_candnbr_relu_p_kernel(tc, x_words, x_scales, w1, w2, gs, pri, of
             planes = sb(name, [P, PACK, c1 - c0], BF16, tag=tag)
             for t in range(PACK):
                 nc.vector.tensor_copy(planes[:, t, :], h[t][:].indirect(nb_t[:, c0 // 16 : c1 // 16]))
-            nc.scalar.copy(out=zi[:, c0:c1, :].rearrange("p (c i) t -> p c t i", i=4), in_=planes[:].rearrange("p t (c i) -> p c t i", i=4))
+            for a in range(c0, c1, PART):
+                nc.scalar.copy(out=zi[:, a : a + PART, :].rearrange("p (c i) t -> p c t i", i=4), in_=planes[:, :, a - c0 : a - c0 + PART].rearrange("p t (c i) -> p c t i", i=4))
 
         def quant_z(c0, c1):
             quantise(z_c[:, c0:c1], z_s[:, c0:c1], zi[:, c0:c1, :].rearrange("p c t -> p (c t)"))
@@ -141,23 +142,23 @@ def tile_picked_candnbr_relu_p_kernel(tc, x_words, x_scales, w1, w2, gs, pri, of
 
         def score(u):
             quantise(z2_c[u][:], z2_s[u][:], z2[u][:].rearrange("p n t -> p (n t)"))
-            for pair in range(2):
-                bank = psum.tile([P, 2, HALF], F32, name="wide")
-                for a in range(2):
-                    vc = slice(HALF * pair + P * a, HALF * pair + P * (a + 1))
-                    product(bank[:, a, :], xc_w[:, vc], xc_s[:, vc], z2_c[u][:], z2_s[u][:])
-                third[u, pair] = bank
+            for v in range(PACK):
+                vc = slice(P * v, P * (v + 1))
+                bank = psum.tile([P, HALF], F32, name="third", tag="wide" if u == 0 else "second")
+                product(bank[:], xc_w[:, vc], xc_s[:, vc], z2_c[u][:], z2_s[u][:])
+                third[u, v] = bank
 
-        def finish(u, pair):
-            res = sb("res%d_%d" % (u, pair), [P, 2, HALF], F32)
-            nc.vector.scalar_tensor_tensor(out=res[:], in0=third[u, pair][:], scalar=0.0625, in1=pri_t[u][:, 2 * pair : 2 * pair + 2, :], op0=ALU.mult, op1=ALU.add)
-            nc.sync.dma_start(out=out.rearrange("(v p) s -> p v s", p=P)[:, 2 * pair : 2 * pair + 2, HALF * u : HALF * (u + 1)], in_=res[:])
+        def finish(u, v):
+            res = sb("res%d_%d" % (u, v), [P, HALF], F32)
+            nc.vector.scalar_tensor_tensor(out=res[:], in0=third[u, v][:], scalar=0.0625, in1=pri_t[u][:, v, :], op0=ALU.mult, op1=ALU.add)
+            nc.sync.dma_start(out=out[P * v : P * (v + 1), HALF * u : HALF * (u + 1)], in_=res[:])
 
         fetch("zp_a", "zp_a", 0, 256)
-        fetch("zp_b", "w2_b", 256, 384)
+        fetch("zp_b", "zp_b", 256, 384)
         quantise(w2_c[:], w2_s[:], g2[:].rearrange("p t m j -> p (t m j)"))
-        quant_z(0, 256)
+        quant_z(0, 128)
         layer2(0)
+        quant_z(128, 256)
         layer2(1)
         fetch("zp_c", "zp_a", 384, 512)
         quant_z(256, 384)
@@ -171,6 +172,7 @@ def tile_picked_candnbr_relu_p_kernel(tc, x_words, x_scales, w1, w2, gs, pri, of
         weigh(3)
         finish(0, 0)
         score(1)
-        finish(0, 1)
-        finish(1, 0)
-        finish(1, 1)
+        for v in range(1, PACK):
+            finish(0, v)
+        for v in range(PACK):
+            finish(1, v)

from contextlib import ExitStack

import concourse.mybir as mybir

K, T, S, V, H = 512, 2048, 512, 512, 512
FLOPS = 2 * K * H * S + 2 * H * H * S + 2 * K * V * S

F32 = mybir.dt.float32
BF16 = mybir.dt.bfloat16
I32 = mybir.dt.int32
U32 = mybir.dt.uint32
U16 = mybir.dt.uint16
U8 = mybir.dt.uint8
FP8X4 = mybir.dt.float8_e4m3fn_x4
ALU = mybir.AluOpType

P = 128
PACK = 4
HALF = 256
PART = 128


def tile_picked_candnbr_relu_p_kernel(tc, x_words, x_scales, w1, w2, gs, pri, offs, nb, cand, out):
    nc = tc.nc
    with ExitStack() as ctx:
        keep = ctx.enter_context(tc.tile_pool(name="keep", bufs=1))
        psum = ctx.enter_context(tc.psum_pool(name="psum", bufs=4))

        def sb(name, shape, dtype, tag=None):
            return keep.tile(shape, dtype, name=name, tag=tag or name, align_bytes=64)

        def load_cols(name, w, c0, c1):
            raw = sb(name, [P, PACK, c1 - c0], F32)
            nc.sync.dma_start(out=raw[:], in_=w.rearrange("(p j) c -> p j c", j=PACK)[:, :, c0:c1])
            return raw

        offs_t = sb("offs_t", [P, S // 16], U16)
        cand_t = sb("cand_t", [P, V // 16], U16)
        nb_t = sb("nb_t", [P, S // 16], U16)
        xw = sb("xw", [P, T], U32)
        xs = sb("xs", [P, T], U8)
        nc.vector.memset(xs[:].bitcast(I32), 0)
        nc.sync.dma_start(offs_t[:], offs)
        nc.sync.dma_start(cand_t[:], cand)
        w1_a = load_cols("w1_a", w1, 0, 256)
        for q in range(4):
            nc.sync.dma_start(out=xs[32 * q : 32 * q + 4, :].bitcast(I32), in_=x_scales[0, 4 * q : 4 * q + 4, :].bitcast(I32))
        w1_b = load_cols("w1_b", w1, 256, 512)
        nc.sync.dma_start(out=xw[:].bitcast(I32), in_=x_words[0].rearrange("p n t -> p (n t)").bitcast(I32))
        nc.sync.dma_start(nb_t[:], nb)
        w2_a = load_cols("w2_a", w2, 0, 128)
        w2_c3 = load_cols("w2_c3", w2, 256, 512)
        w2_b = load_cols("w2_b", w2, 128, 256)
        gs_t = sb("gs_t", [P, PACK], F32)
        nc.sync.dma_start(out=gs_t[:], in_=gs.rearrange("(p t) o -> p (t o)", t=PACK))
        pri_t = []
        for u in range(2):
            pt = sb("pri%d" % u, [P, PACK, HALF], F32)
            nc.sync.dma_start(out=pt[:], in_=pri.rearrange("(v p) s -> p v s", p=P)[:, :, u * HALF : (u + 1) * HALF])
            pri_t.append(pt)

        def deal(copy, grouped, c0, raw):
            m0, m1 = c0 // PACK, (c0 + raw.shape[2]) // PACK
            copy(out=grouped[:, :, m0:m1, :].rearrange("p t m j -> p m j t"), in_=raw.rearrange("p j (m t) -> p m j t", t=PACK))

        def quantise(codes, scales, values):
            nc.vector.quantize_mx(out=codes.bitcast(FP8X4), scales=scales, in_=values)

        def product(acc, lhs_c, lhs_s, rhs_c, rhs_s):
            nc.tensor.matmul_mx(out=acc, lhsT=lhs_c.bitcast(FP8X4), lhsT_scale=lhs_s, rhs=rhs_c.bitcast(FP8X4), rhs_scale=rhs_s, start=True, stop=True)

        xq_w = sb("xq_w", [P, S], U32)
        xq_s = sb("xq_s", [P, S], U8)
        xc_s = sb("xc_s", [P, V], U8)
        nc.vector.tensor_copy(xq_s[:], xs[:].indirect(offs_t[:]))
        nc.vector.tensor_copy(xc_s[:], xs[:].indirect(cand_t[:]))

        g1 = sb("g1", [P, PACK, P, PACK], BF16)
        deal(nc.scalar.copy, g1, 0, w1_a[:])
        deal(nc.scalar.copy, g1, 256, w1_b[:])
        w1_c = sb("w1_c", [P, H], U32)
        w1_s = sb("w1_s", [P, H], U8)
        quantise(w1_c[:], w1_s[:], g1[:].rearrange("p t m j -> p (t m j)"))
        for u in range(2):
            nc.vector.tensor_copy(xq_w[:, HALF * u : HALF * (u + 1)], xw[:].indirect(offs_t[:, 16 * u : 16 * (u + 1)]))
        xc_w = sb("xc_w", [P, V], U32)
        nc.vector.tensor_copy(xc_w[:], xw[:].indirect(cand_t[:]))

        g2 = sb("g2", [P, PACK, P, PACK], BF16)
        deal(nc.scalar.copy, g2, 0, w2_a[:])
        h = []
        for t in range(PACK):
            cols = slice(P * t, P * (t + 1))
            ht = sb("h%d" % t, [P, S], F32)
            edges = (0, 256, 384, 512) if t == 0 else (0, 512)
            for c0, c1 in zip(edges, edges[1:]):
                bank = psum.tile([P, c1 - c0], F32, name="first", tag="wide" if c1 - c0 > PART else "second")
                product(bank[:], w1_c[:, cols], w1_s[:, cols], xq_w[:, c0:c1], xq_s[:, c0:c1])
                nc.scalar.copy(out=ht[:, c0:c1], in_=bank[:])
            h.append(ht)

        deal(nc.scalar.copy, g2, 128, w2_b[:])
        deal(nc.scalar.copy, g2, 256, w2_c3[:])

        w2_c = sb("w2_c", [P, H], U32)
        w2_s = sb("w2_s", [P, H], U8)
        zi = sb("zi", [P, S, PACK], BF16)
        z_c = sb("z_c", [P, S], U32)
        z_s = sb("z_s", [P, S], U8)

        def fetch(name, tag, c0, c1):
            planes = sb(name, [P, PACK, c1 - c0], BF16, tag=tag)
            for t in range(PACK):
                nc.vector.tensor_copy(planes[:, t, :], h[t][:].indirect(nb_t[:, c0 // 16 : c1 // 16]))
            for a in range(c0, c1, PART):
                nc.scalar.copy(out=zi[:, a : a + PART, :].rearrange("p (c i) t -> p c t i", i=4), in_=planes[:, :, a - c0 : a - c0 + PART].rearrange("p t (c i) -> p c t i", i=4))

        def quant_z(c0, c1):
            quantise(z_c[:, c0:c1], z_s[:, c0:c1], zi[:, c0:c1, :].rearrange("p c t -> p (c t)"))

        second = {}

        def layer2(c):
            cols = slice(PART * c, PART * (c + 1))
            bank = psum.tile([P, PACK, PART], F32, name="second")
            for t in range(PACK):
                wc = slice(P * t, P * (t + 1))
                product(bank[:, t, :], w2_c[:, wc], w2_s[:, wc], z_c[:, cols], z_s[:, cols])
            second[c] = bank

        z2 = [sb("z2_%d" % u, [P, HALF, PACK], BF16) for u in range(2)]
        z2_c = [sb("z2_c%d" % u, [P, HALF], U32) for u in range(2)]
        z2_s = [sb("z2_s%d" % u, [P, HALF], U8) for u in range(2)]

        def weigh(c):
            u, a = divmod(c, 2)
            nc.vector.scalar_tensor_tensor(
                out=z2[u][:, PART * a : PART * (a + 1), :], in0=second[c][:].rearrange("p t n -> p n t"), scalar=0.0,
                in1=gs_t[:].unsqueeze(1).to_broadcast([P, PART, PACK]), op0=ALU.max, op1=ALU.mult)

        third = {}

        def score(u):
            quantise(z2_c[u][:], z2_s[u][:], z2[u][:].rearrange("p n t -> p (n t)"))
            for v in range(PACK):
                vc = slice(P * v, P * (v + 1))
                bank = psum.tile([P, HALF], F32, name="third", tag="wide" if u == 0 else "second")
                product(bank[:], xc_w[:, vc], xc_s[:, vc], z2_c[u][:], z2_s[u][:])
                third[u, v] = bank

        def finish(u, v):
            res = sb("res%d_%d" % (u, v), [P, HALF], F32)
            nc.vector.scalar_tensor_tensor(out=res[:], in0=third[u, v][:], scalar=0.0625, in1=pri_t[u][:, v, :], op0=ALU.mult, op1=ALU.add)
            nc.sync.dma_start(out=out[P * v : P * (v + 1), HALF * u : HALF * (u + 1)], in_=res[:])

        fetch("zp_a", "zp_a", 0, 256)
        fetch("zp_b", "zp_b", 256, 384)
        quantise(w2_c[:], w2_s[:], g2[:].rearrange("p t m j -> p (t m j)"))
        quant_z(0, 128)
        layer2(0)
        quant_z(128, 256)
        layer2(1)
        fetch("zp_c", "zp_a", 384, 512)
        quant_z(256, 384)
        layer2(2)
        weigh(0)
        weigh(1)
        quant_z(384, 512)
        layer2(3)
        score(0)
        weigh(2)
        weigh(3)
        finish(0, 0)
        score(1)
        for v in range(1, PACK):
            finish(0, v)
        for v in range(PACK):
            finish(1, v)
